import numpy as np
import ml_dtypes


def mxq(x, axis, fmt="e4m3"):
    dtype, down = {"e4m3": (ml_dtypes.float8_e4m3fn, 7), "e5m2": (ml_dtypes.float8_e5m2, 14)}[fmt]
    v = np.moveaxis(np.asarray(x, np.float32).astype(ml_dtypes.bfloat16).astype(np.float64), axis, -1)
    blocks = v.reshape(v.shape[:-1] + (-1, 32))
    amax = np.abs(blocks).max(-1, keepdims=True)
    byte = np.maximum(np.where(amax > 0, np.frexp(amax)[1] - 1 + 127, 0) - down, 1)
    scale = np.exp2(byte - 127.0)
    codes = (blocks / scale).astype(np.float32).astype(dtype).astype(np.float64)
    return np.moveaxis((codes * scale).reshape(v.shape), -1, axis)


WIDE = False


def mx_kscale(k):
    if not WIDE:
        return np.ones(k)
    levels = np.array([10, -10, 5, -5, 0])
    if k % 512:
        return np.exp2(np.random.permutation(np.resize(levels, k // 32))).repeat(32)
    a = np.empty((k // 512, 16))
    for p in range(k // 512):
        a[p, :8] = np.random.permutation(np.resize(levels, 8))
        for g in range(8):
            far = levels[np.abs(levels - a[p, g]) >= 10]
            a[p, g + 8] = far[np.random.randint(len(far))]
    return np.exp2(a.ravel()).repeat(32)


def f64(x):
    return np.asarray(x).astype(np.float64)


def striped(idx):
    return np.tile(np.asarray(idx).reshape(-1, 16).T, (8, 1)).astype(np.uint16)


def unstriped(offs):
    return offs[:16].T.reshape(-1).astype(np.int64)


E2M1 = np.array([0.0, 0.5, 1.0, 1.5, 2.0, 3.0, 4.0, 6.0, -0.0, -0.5, -1.0, -1.5, -2.0, -3.0, -4.0, -6.0])


def pack_weight(w, fmt):
    k, n = w.shape
    w = f64(np.asarray(w, np.float32).astype(ml_dtypes.bfloat16)).reshape(k // 32, 32, n)
    amax = np.abs(w).max(1)
    if fmt == "e4m3":
        byte = np.frexp(amax)[1] - 1 + 127 - 7
    else:
        mant, ex = np.frexp(amax / 6.0)
        byte = np.where(mant > 0.5, ex, ex - 1) + 127
    byte = np.clip(np.where(amax > 0, byte, 1), 1, 254)
    scaled = (w * np.exp2(127.0 - byte)[:, None, :]).reshape(k, n).astype(np.float32)
    by_word = np.ascontiguousarray(scaled.reshape(k // 512, 128, 4, n).transpose(0, 1, 3, 2))
    if fmt == "e4m3":
        words = by_word.astype(ml_dtypes.float8_e4m3fn).view(np.uint8)
    else:
        c = by_word.astype(ml_dtypes.float4_e2m1fn).view(np.uint8) & 0xF
        words = (c[..., 0::2] | (c[..., 1::2] << 4)).reshape(k // 512, 128, 2 * n)
    return np.ascontiguousarray(words), np.ascontiguousarray(byte.astype(np.uint8).reshape(k // 512, 16, n))


def unpack_weight(words, scales, fmt):
    g, _, n = scales.shape
    words = np.ascontiguousarray(words).reshape(g, 128, n, -1)
    if fmt == "e4m3":
        vals = words.view(ml_dtypes.float8_e4m3fn).astype(np.float64)
    else:
        nib = np.empty((g, 128, n, 4), np.uint8)
        nib[..., 0::2] = words & 0xF
        nib[..., 1::2] = words >> 4
        vals = E2M1[nib]
    vals = vals * np.repeat(np.exp2(scales.astype(np.float64) - 127.0), 8, axis=1)[..., None]
    return vals.transpose(0, 1, 3, 2).reshape(g * 512, n)


def sigmoid(v):
    return 1.0 / (1.0 + np.exp(-v))


D, E, T, I, Q, G, U = 512, 512, 2048, 512, 128, 64, 256


def setup_inputs():
    n = np.random.standard_normal
    idx2 = np.random.permutation(U)[:G]
    idx = np.random.permutation(T)[:I]
    fd = mx_kscale(D)
    fe = mx_kscale(E)
    keysp = pack_weight(n((D, T)) / fd[:, None], "e2m1")
    valsp = pack_weight(n((E, T)) / fe[:, None], "e2m1")
    return {
        "query": (n((D, Q)) * 0.7 / np.sqrt(D) * fd[:, None]).astype(np.float32),
        "pquery": (n((D, Q)) * 1.0 / np.sqrt(D) * fd[:, None]).astype(np.float32),
        "keys_words": keysp[0],
        "keys_scales": keysp[1],
        "pgsum": (n((D, U)) / fd[:, None]).astype(np.float32),
        "reserve": (np.random.uniform(20.0, 100.0, (Q, 1))).astype(np.float32),
        "gout": (n((E, Q)) * 1 / np.sqrt(E) * fe[:, None]).astype(np.float32),
        "vals_words": valsp[0],
        "vals_scales": valsp[1],
        "dquery": (n((D, Q)) * 1.0 / np.sqrt(D) * fd[:, None]).astype(np.float32),
        "base": (0.5 * n((Q, T))).astype(np.float32),
        "offs2": striped(idx2),
        "offs": striped(idx),
    }


def reference(query, pquery, keys_words, keys_scales, pgsum, reserve, gout, vals_words, vals_scales, dquery, base, offs2, offs):
    idx2 = unstriped(offs2)
    idx = unstriped(offs)
    keysu = unpack_weight(keys_words, keys_scales, "e2m1")
    valsu = unpack_weight(vals_words, vals_scales, "e2m1")
    pqueryq = mxq(f64(pquery), 0, "e4m3")
    pgsumidx2q = mxq(f64(pgsum)[:, idx2], 0, "e4m3")
    h0 = pqueryq.T @ pgsumidx2q
    g1 = sigmoid(h0)
    gr = np.repeat(g1, I // G, axis=1)
    queryq = mxq(f64(query), 0, "e4m3")
    keysidxg = keysu[:, idx]
    a = queryq.T @ keysidxg
    dqueryq = mxq(f64(dquery), 0, "e4m3")
    ta = dqueryq.T @ keysidxg
    p = np.exp(a) * gr
    z = np.sum(p, axis=1, keepdims=True) + f64(reserve)
    goutq = mxq(f64(gout), 0, "e4m3")
    valsidxg = valsu[:, idx]
    c0 = goutq.T @ valsidxg
    dz = np.sum(c0 * p / np.square(z) * (-1.0), axis=1, keepdims=True)
    dp = c0 / z + dz
    tp = ta * np.exp(a) * gr
    tz = np.sum(tp, axis=1, keepdims=True)
    tdz = np.sum((tp * c0 - tz * z * 2.0 * c0 * p / np.square(z)) / np.square(z) * (-1.0), axis=1, keepdims=True)
    tdp = tz * c0 / np.square(z) * (-1.0) + tdz
    tda = tdp * gr * np.exp(a) + ta * np.exp(a) * dp * gr
    gs = tda * 512.0
    gf = np.zeros((Q, T))
    gf[:, idx] = gs
    y = f64(base) + gf
    return y

@@ -1,0 +1,180 @@
+from contextlib import ExitStack
+
+import concourse.mybir as mybir
+
+F32 = mybir.dt.float32
+BF16 = mybir.dt.bfloat16
+I32 = mybir.dt.int32
+U32 = mybir.dt.uint32
+U16 = mybir.dt.uint16
+U8 = mybir.dt.uint8
+FP8X4 = mybir.dt.float8_e4m3fn_x4
+FP4X4 = mybir.dt.float4_e2m1fn_x4
+ACT = mybir.ActivationFunctionType
+ALU = mybir.AluOpType
+
+P = 128
+PACK = 4
+T = 2048
+SLOTS = 512
+PAGES = 64
+PAGE_SLOTS = SLOTS // PAGES
+TABLE = 256
+GAIN = 512.0
+STORE_WIDTHS = (256, 512, 512, 512, 256)
+
+FLOPS = 2 * 512 * P * (3 * SLOTS + PAGES)
+
+
+def tile_attend_hvpagetablegate_s_kernel(tc, query, pquery, keys_words, keys_scales, pgsum, reserve, gout,
+                                          vals_words, vals_scales, dquery, base, offs2, offs, out):
+    nc = tc.nc
+    with ExitStack() as ctx:
+        sb = ctx.enter_context(tc.tile_pool(name="sb", bufs=1))
+        ps = ctx.enter_context(tc.psum_pool(name="ps", bufs=1))
+
+        def load_words(words, name):
+            tile = sb.tile([P, T], U16, name=name, align_bytes=64)
+            nc.sync.dma_start(out=tile[:].bitcast(I32), in_=words[0].bitcast(I32))
+            return tile
+
+        def zeroed_scales(name):
+            tile = sb.tile([P, T], U8, name=name, tag=name, align_bytes=64)
+            nc.gpsimd.memset(tile[:].bitcast(I32), 0)
+            return tile
+
+        def load_scales(queue, tile, scales):
+            for r in range(PACK):
+                queue.dma_start(out=tile[:].bitcast(I32)[r:P:32, :], in_=scales[0].bitcast(I32)[r:16:PACK, :])
+
+        def load_rows(rows, name):
+            tile = sb.tile([P, PACK, rows.shape[1]], F32, name=name, align_bytes=64)
+            nc.sync.dma_start(out=tile[:], in_=rows.rearrange("(p t) c -> p t c", t=PACK))
+            return tile
+
+        def gather(window, dtype, name):
+            tile = sb.tile([P, SLOTS], dtype, name=name, align_bytes=64)
+            nc.vector.tensor_copy(tile[:], window[:].indirect(slot_list[:]))
+            return tile
+
+        def quantize(planes, name):
+            width = planes.shape[2]
+            woven = sb.tile([P, width, PACK], BF16, name=name + "_bf", tag=name + "_bf", align_bytes=64)
+            nc.scalar.copy(out=woven[:].rearrange("p (c i) t -> p c t i", i=4),
+                           in_=planes[:].rearrange("p t (c i) -> p c t i", i=4))
+            codes = sb.tile([P, width], U32, name=name + "_codes", align_bytes=64)
+            scales = sb.tile([P, width], U8, name=name + "_scales", align_bytes=64)
+            nc.vector.quantize_mx(out=codes[:].bitcast(FP8X4), scales=scales[:],
+                                  in_=woven[:].rearrange("p c t -> p (c t)"))
+            return codes, scales
+
+        def product(rows, moving, moving_scales, name):
+            codes, scales = rows
+            acc = ps.tile([P, moving_scales.shape[1]], F32, name=name)
+            nc.tensor.matmul_mx(out=acc[:], lhsT=codes[:].bitcast(FP8X4), lhsT_scale=scales[:],
+                                rhs=moving, rhs_scale=moving_scales[:], start=True, stop=True)
+            return acc
+
+        def wide(name):
+            return sb.tile([P, SLOTS], F32, name=name, align_bytes=64)
+
+        def column(name, n=1):
+            return sb.tile([P, n], F32, name=name)
+
+        key_scale_pool = zeroed_scales("key_scale_pool")
+        val_scale_pool = zeroed_scales("val_scale_pool")
+        scattered = sb.tile([P, T], F32, name="scattered", align_bytes=64)
+        nc.vector.memset(scattered[:], 0.0)
+        tz_pair = column("tz_pair", 2)
+        nc.vector.memset(tz_pair[:, 1:2], -1.0 / GAIN)
+
+        slot_list = sb.tile([P, SLOTS // 16], U16, name="slot_list")
+        nc.sync.dma_start(slot_list[:], offs)
+        key_word_pool = load_words(keys_words, "key_word_pool")
+        load_scales(nc.scalar, key_scale_pool, keys_scales)
+        pgsum_rows = load_rows(pgsum, "pgsum_rows")
+        page_list = sb.tile([P, PAGES // 16], U16, name="page_list")
+        nc.sync.dma_start(page_list[:], offs2)
+        pquery_rows = load_rows(pquery, "pquery_rows")
+        query_rows = load_rows(query, "query_rows")
+        val_word_pool = load_words(vals_words, "val_word_pool")
+        reserve_col = column("reserve_col")
+        nc.sync.dma_start(out=reserve_col[:], in_=reserve)
+        dquery_rows = load_rows(dquery, "dquery_rows")
+        load_scales(nc.sync, val_scale_pool, vals_scales)
+        gout_rows = load_rows(gout, "gout_rows")
+        base_rows = sb.tile([P, T], F32, name="base_rows", align_bytes=64)
+        nc.sync.dma_start(out=base_rows[:], in_=base)
+
+        key_words = gather(key_word_pool, U16, "key_words")
+        key_scales = gather(key_scale_pool, U8, "key_scales")
+        page_planes = sb.tile([P, PACK, PAGES], F32, name="page_planes", align_bytes=64)
+        for t in range(PACK):
+            nc.vector.tensor_copy(page_planes[:, t, :], pgsum_rows[:, t, :].indirect(page_list[:]))
+
+        pquery_mx = quantize(pquery_rows, "pquery")
+        query_mx = quantize(query_rows, "query")
+        page_codes, page_scales = quantize(page_planes, "pages")
+        a = product(query_mx, key_words[:].bitcast(FP4X4), key_scales, "a")
+        h0 = product(pquery_mx, page_codes[:].bitcast(FP8X4), page_scales, "h0")
+
+        val_words = gather(val_word_pool, U16, "val_words")
+
+        h_abs = column("h_abs", PAGES)
+        h_neg = column("h_neg", PAGES)
+        h_tanh = column("h_tanh", PAGES)
+        h_exp = column("h_exp", PAGES)
+        nc.scalar.activation(h_abs[:], h0[:], ACT.Abs)
+        nc.scalar.activation(h_neg[:], h0[:], ACT.Relu, scale=-1.0)
+        nc.scalar.activation(h_tanh[:], h_abs[:], ACT.Tanh, scale=0.5)
+        nc.scalar.activation(h_exp[:], h_neg[:], ACT.Exp, scale=-1.0)
+        exp_a = wide("exp_a")
+        nc.scalar.activation(exp_a[:], a[:], ACT.Exp)
+        reserve_scaled = column("reserve_scaled")
+        nc.scalar.activation(reserve_scaled[:], reserve_col[:], ACT.Copy, scale=2.0 / GAIN)
+
+        dquery_mx = quantize(dquery_rows, "dquery")
+        ta = product(dquery_mx, key_words[:].bitcast(FP4X4), key_scales, "ta")
+        val_scales = gather(val_scale_pool, U8, "val_scales")
+        gout_mx = quantize(gout_rows, "gout")
+        c0 = product(gout_mx, val_words[:].bitcast(FP4X4), val_scales, "c0")
+
+        gate2 = sb.tile([P, PAGES], F32, name="gate2", tag="gout_bf", align_bytes=64)
+        nc.vector.scalar_tensor_tensor(gate2[:], h_tanh[:], 1.0, h_exp[:], ALU.add, ALU.mult)
+
+        p2 = sb.tile([P, SLOTS], F32, name="p2", tag="val_scale_pool", align_bytes=64)
+        p2_sum = column("p2_sum")
+        nc.vector.scalar_tensor_tensor(
+            p2[:].rearrange("p (g j) -> p g j", j=PAGE_SLOTS), exp_a[:].rearrange("p (g j) -> p g j", j=PAGE_SLOTS), 1.0,
+            gate2[:].unsqueeze(2).to_broadcast([P, PAGES, PAGE_SLOTS]), ALU.mult, ALU.mult, accum_out=p2_sum[:])
+        z_scaled = column("z_scaled")
+        nc.scalar.activation(z_scaled[:], p2_sum[:], ACT.Identity, scale=1.0 / GAIN, bias=reserve_scaled[:])
+        tp = wide("tp")
+        nc.vector.scalar_tensor_tensor(tp[:], ta[:], 1.0 / GAIN, p2[:], ALU.mult, ALU.mult, accum_out=tz_pair[:, 0:1])
+        row = column("row", 3)
+        s, mu, neg_rz = row[:, 0:1], row[:, 1:2], row[:, 2:3]
+        nc.vector.reciprocal(s, z_scaled[:])
+        nc.scalar.activation(row[:, 1:3], tz_pair[:], ACT.Copy, scale=s)
+        pc = wide("pc")
+        nu = column("nu")
+        nc.vector.scalar_tensor_tensor(pc[:], c0[:], s, p2[:], ALU.mult, ALU.mult, accum_out=nu[:])
+        by_nu = column("by_nu", 2)
+        nc.scalar.activation(by_nu[:], row[:, 0:2], ACT.Copy, scale=nu[:])
+        tp_nu = wide("tp_nu")
+        nc.scalar.activation(tp_nu[:], tp[:], ACT.Copy, scale=by_nu[:, 0:1])
+        cross = wide("cross")
+        cross_sum = column("cross_sum")
+        nc.vector.scalar_tensor_tensor(cross[:], ta[:], mu, pc[:], ALU.subtract, ALU.mult, accum_out=cross_sum[:])
+        kappa = column("kappa")
+        nc.vector.tensor_scalar(kappa[:], cross_sum[:], by_nu[:, 1:2], neg_rz, ALU.subtract, ALU.mult)
+        rest = wide("rest")
+        nc.vector.scalar_tensor_tensor(rest[:], p2[:], kappa[:], tp_nu[:], ALU.mult, ALU.subtract)
+        nc.vector.tensor_tensor(scattered[:].indirect(slot_list[:]), cross[:], rest[:], ALU.add)
+
+        start = 0
+        for n, width in enumerate(STORE_WIDTHS):
+            cols = slice(start, start + width)
+            result = sb.tile([P, width], F32, name="result%d" % n, align_bytes=64)
+            nc.vector.tensor_tensor(result[:], base_rows[:, cols], scattered[:, cols], ALU.add)
+            nc.sync.dma_start(out=out[:, cols], in_=result[:])
+            start = start + width

@@ -48,7 +48,7 @@ def tile_attend_hvpagetablegate_s_kernel(tc, query, pquery, keys_words, keys_sca
                 queue.dma_start(out=tile[:].bitcast(I32)[r:P:32, :], in_=scales[0].bitcast(I32)[r:16:PACK, :])
 
         def load_rows(rows, name):
-            tile = sb.tile([P, PACK, rows.shape[1]], F32, name=name, align_bytes=64)
+            tile = sb.tile([P, PACK, rows.shape[1]], F32, name=name, tag=name, align_bytes=64)
             nc.sync.dma_start(out=tile[:], in_=rows.rearrange("(p t) c -> p t c", t=PACK))
             return tile
 
@@ -57,11 +57,14 @@ def tile_attend_hvpagetablegate_s_kernel(tc, query, pquery, keys_words, keys_sca
             nc.vector.tensor_copy(tile[:], window[:].indirect(slot_list[:]))
             return tile
 
-        def quantize(planes, name):
-            width = planes.shape[2]
-            woven = sb.tile([P, width, PACK], BF16, name=name + "_bf", tag=name + "_bf", align_bytes=64)
+        def weave(planes, name):
+            woven = sb.tile([P, planes.shape[2], PACK], BF16, name=name + "_bf", align_bytes=64)
             nc.scalar.copy(out=woven[:].rearrange("p (c i) t -> p c t i", i=4),
                            in_=planes[:].rearrange("p t (c i) -> p c t i", i=4))
+            return woven
+
+        def quantize(woven, name):
+            width = woven.shape[1]
             codes = sb.tile([P, width], U32, name=name + "_codes", align_bytes=64)
             scales = sb.tile([P, width], U8, name=name + "_scales", align_bytes=64)
             nc.vector.quantize_mx(out=codes[:].bitcast(FP8X4), scales=scales[:],
@@ -91,62 +94,62 @@ def tile_attend_hvpagetablegate_s_kernel(tc, query, pquery, keys_words, keys_sca
         slot_list = sb.tile([P, SLOTS // 16], U16, name="slot_list")
         nc.sync.dma_start(slot_list[:], offs)
         key_word_pool = load_words(keys_words, "key_word_pool")
-        load_scales(nc.scalar, key_scale_pool, keys_scales)
+        load_scales(nc.sync, key_scale_pool, keys_scales)
+        query_rows = load_rows(query, "query_rows")
+        pquery_rows = load_rows(pquery, "pquery_rows")
         pgsum_rows = load_rows(pgsum, "pgsum_rows")
         page_list = sb.tile([P, PAGES // 16], U16, name="page_list")
         nc.sync.dma_start(page_list[:], offs2)
-        pquery_rows = load_rows(pquery, "pquery_rows")
-        query_rows = load_rows(query, "query_rows")
         val_word_pool = load_words(vals_words, "val_word_pool")
+        load_scales(nc.sync, val_scale_pool, vals_scales)
+        dquery_rows = load_rows(dquery, "dquery_rows")
+        gout_rows = load_rows(gout, "gout_rows")
         reserve_col = column("reserve_col")
         nc.sync.dma_start(out=reserve_col[:], in_=reserve)
-        dquery_rows = load_rows(dquery, "dquery_rows")
-        load_scales(nc.sync, val_scale_pool, vals_scales)
-        gout_rows = load_rows(gout, "gout_rows")
         base_rows = sb.tile([P, T], F32, name="base_rows", align_bytes=64)
         nc.sync.dma_start(out=base_rows[:], in_=base)
 
         key_words = gather(key_word_pool, U16, "key_words")
         key_scales = gather(key_scale_pool, U8, "key_scales")
-        page_planes = sb.tile([P, PACK, PAGES], F32, name="page_planes", align_bytes=64)
+        query_mx = quantize(weave(query_rows, "query"), "query")
+        pquery_mx = quantize(weave(pquery_rows, "pquery"), "pquery")
+        pages_bf = sb.tile([P, PAGES, PACK], BF16, name="pages_bf", align_bytes=64)
         for t in range(PACK):
-            nc.vector.tensor_copy(page_planes[:, t, :], pgsum_rows[:, t, :].indirect(page_list[:]))
+            nc.vector.tensor_copy(pages_bf[:, :, t], pgsum_rows[:, t, :].indirect(page_list[:]))
 
-        pquery_mx = quantize(pquery_rows, "pquery")
-        query_mx = quantize(query_rows, "query")
-        page_codes, page_scales = quantize(page_planes, "pages")
+        page_codes, page_scales = quantize(pages_bf, "pages")
         a = product(query_mx, key_words[:].bitcast(FP4X4), key_scales, "a")
         h0 = product(pquery_mx, page_codes[:].bitcast(FP8X4), page_scales, "h0")
 
         val_words = gather(val_word_pool, U16, "val_words")
+        val_scales = gather(val_scale_pool, U8, "val_scales")
 
+        exp_a = wide("exp_a")
+        nc.scalar.activation(exp_a[:], a[:], ACT.Exp)
+        dquery_bf = weave(dquery_rows, "dquery")
+        gout_bf = weave(gout_rows, "gout")
         h_abs = column("h_abs", PAGES)
         h_neg = column("h_neg", PAGES)
         h_tanh = column("h_tanh", PAGES)
-        h_exp = column("h_exp", PAGES)
+        h_exp = sb.tile([P, PAGES], F32, name="h_exp", tag="gout_rows", align_bytes=64)
         nc.scalar.activation(h_abs[:], h0[:], ACT.Abs)
         nc.scalar.activation(h_neg[:], h0[:], ACT.Relu, scale=-1.0)
         nc.scalar.activation(h_tanh[:], h_abs[:], ACT.Tanh, scale=0.5)
         nc.scalar.activation(h_exp[:], h_neg[:], ACT.Exp, scale=-1.0)
-        exp_a = wide("exp_a")
-        nc.scalar.activation(exp_a[:], a[:], ACT.Exp)
         reserve_scaled = column("reserve_scaled")
         nc.scalar.activation(reserve_scaled[:], reserve_col[:], ACT.Copy, scale=2.0 / GAIN)
 
-        dquery_mx = quantize(dquery_rows, "dquery")
-        ta = product(dquery_mx, key_words[:].bitcast(FP4X4), key_scales, "ta")
-        val_scales = gather(val_scale_pool, U8, "val_scales")
-        gout_mx = quantize(gout_rows, "gout")
-        c0 = product(gout_mx, val_words[:].bitcast(FP4X4), val_scales, "c0")
+        ta = product(quantize(dquery_bf, "dquery"), key_words[:].bitcast(FP4X4), key_scales, "ta")
+        c0 = product(quantize(gout_bf, "gout"), val_words[:].bitcast(FP4X4), val_scales, "c0")
 
-        gate2 = sb.tile([P, PAGES], F32, name="gate2", tag="gout_bf", align_bytes=64)
+        gate2 = column("gate2", PAGES)
         nc.vector.scalar_tensor_tensor(gate2[:], h_tanh[:], 1.0, h_exp[:], ALU.add, ALU.mult)
-
-        p2 = sb.tile([P, SLOTS], F32, name="p2", tag="val_scale_pool", align_bytes=64)
+        p2 = wide("p2")
         p2_sum = column("p2_sum")
         nc.vector.scalar_tensor_tensor(
             p2[:].rearrange("p (g j) -> p g j", j=PAGE_SLOTS), exp_a[:].rearrange("p (g j) -> p g j", j=PAGE_SLOTS), 1.0,
             gate2[:].unsqueeze(2).to_broadcast([P, PAGES, PAGE_SLOTS]), ALU.mult, ALU.mult, accum_out=p2_sum[:])
+
         z_scaled = column("z_scaled")
         nc.scalar.activation(z_scaled[:], p2_sum[:], ACT.Identity, scale=1.0 / GAIN, bias=reserve_scaled[:])
         tp = wide("tp")

@@ -15,15 +15,19 @@ ALU = mybir.AluOpType
 
 P = 128
 PACK = 4
-T = 2048
+K = P * PACK
+BLOCKS = K // 32
+QUADRANT = 32
+LIST_ROWS = 16
+RUN = 4
+TOKENS = 2048
 SLOTS = 512
 PAGES = 64
 PAGE_SLOTS = SLOTS // PAGES
-TABLE = 256
 GAIN = 512.0
 STORE_WIDTHS = (256, 512, 512, 512, 256)
 
-FLOPS = 2 * 512 * P * (3 * SLOTS + PAGES)
+FLOPS = 2 * K * P * (3 * SLOTS + PAGES)
 
 
 def tile_attend_hvpagetablegate_s_kernel(tc, query, pquery, keys_words, keys_scales, pgsum, reserve, gout,
@@ -34,33 +38,34 @@ def tile_attend_hvpagetablegate_s_kernel(tc, query, pquery, keys_words, keys_sca
         ps = ctx.enter_context(tc.psum_pool(name="ps", bufs=1))
 
         def load_words(words, name):
-            tile = sb.tile([P, T], U16, name=name, align_bytes=64)
+            tile = sb.tile([P, TOKENS], U16, name=name, align_bytes=64)
             nc.sync.dma_start(out=tile[:].bitcast(I32), in_=words[0].bitcast(I32))
             return tile
 
         def zeroed_scales(name):
-            tile = sb.tile([P, T], U8, name=name, tag=name, align_bytes=64)
+            tile = sb.tile([P, TOKENS], U8, name=name, tag=name, align_bytes=64)
             nc.gpsimd.memset(tile[:].bitcast(I32), 0)
             return tile
 
-        def load_scales(queue, tile, scales):
+        def load_scales(tile, scales):
             for r in range(PACK):
-                queue.dma_start(out=tile[:].bitcast(I32)[r:P:32, :], in_=scales[0].bitcast(I32)[r:16:PACK, :])
+                nc.sync.dma_start(out=tile[:].bitcast(I32)[r:P:QUADRANT, :],
+                                  in_=scales[0].bitcast(I32)[r:BLOCKS:PACK, :])
 
         def load_rows(rows, name):
             tile = sb.tile([P, PACK, rows.shape[1]], F32, name=name, tag=name, align_bytes=64)
             nc.sync.dma_start(out=tile[:], in_=rows.rearrange("(p t) c -> p t c", t=PACK))
             return tile
 
-        def gather(window, dtype, name):
-            tile = sb.tile([P, SLOTS], dtype, name=name, align_bytes=64)
+        def gather(window, dtype, name, tag):
+            tile = sb.tile([P, SLOTS], dtype, name=name, tag=tag, align_bytes=64)
             nc.vector.tensor_copy(tile[:], window[:].indirect(slot_list[:]))
             return tile
 
         def weave(planes, name):
-            woven = sb.tile([P, planes.shape[2], PACK], BF16, name=name + "_bf", align_bytes=64)
-            nc.scalar.copy(out=woven[:].rearrange("p (c i) t -> p c t i", i=4),
-                           in_=planes[:].rearrange("p t (c i) -> p c t i", i=4))
+            woven = sb.tile([P, planes.shape[2], PACK], BF16, name=name + "_bf", tag=name + "_bf", align_bytes=64)
+            nc.scalar.copy(out=woven[:].rearrange("p (c i) t -> p c t i", i=RUN),
+                           in_=planes[:].rearrange("p t (c i) -> p c t i", i=RUN))
             return woven
 
         def quantize(woven, name):
@@ -71,113 +76,107 @@ def tile_attend_hvpagetablegate_s_kernel(tc, query, pquery, keys_words, keys_sca
                                   in_=woven[:].rearrange("p c t -> p (c t)"))
             return codes, scales
 
-        def product(rows, moving, moving_scales, name):
-            codes, scales = rows
+        def product(stationary, moving, moving_scales, name):
+            codes, scales = stationary
             acc = ps.tile([P, moving_scales.shape[1]], F32, name=name)
             nc.tensor.matmul_mx(out=acc[:], lhsT=codes[:].bitcast(FP8X4), lhsT_scale=scales[:],
                                 rhs=moving, rhs_scale=moving_scales[:], start=True, stop=True)
             return acc
 
-        def wide(name):
+        def by_slot(name):
             return sb.tile([P, SLOTS], F32, name=name, align_bytes=64)
 
-        def column(name, n=1):
+        def columns(name, n=1):
             return sb.tile([P, n], F32, name=name)
 
         key_scale_pool = zeroed_scales("key_scale_pool")
         val_scale_pool = zeroed_scales("val_scale_pool")
-        scattered = sb.tile([P, T], F32, name="scattered", align_bytes=64)
+        scattered = sb.tile([P, TOKENS], F32, name="scattered", align_bytes=64)
         nc.vector.memset(scattered[:], 0.0)
-        tz_pair = column("tz_pair", 2)
-        nc.vector.memset(tz_pair[:, 1:2], -1.0 / GAIN)
+        tz_row = columns("tz_row", 3)
+        nc.vector.memset(tz_row[:, 1:2], -1.0)
+        nc.vector.memset(tz_row[:, 2:3], GAIN)
 
-        slot_list = sb.tile([P, SLOTS // 16], U16, name="slot_list")
+        slot_list = sb.tile([P, SLOTS // LIST_ROWS], U16, name="slot_list")
         nc.sync.dma_start(slot_list[:], offs)
         key_word_pool = load_words(keys_words, "key_word_pool")
-        load_scales(nc.sync, key_scale_pool, keys_scales)
-        query_rows = load_rows(query, "query_rows")
-        pquery_rows = load_rows(pquery, "pquery_rows")
+        load_scales(key_scale_pool, keys_scales)
         pgsum_rows = load_rows(pgsum, "pgsum_rows")
-        page_list = sb.tile([P, PAGES // 16], U16, name="page_list")
+        page_list = sb.tile([P, PAGES // LIST_ROWS], U16, name="page_list")
         nc.sync.dma_start(page_list[:], offs2)
+        pquery_rows = load_rows(pquery, "pquery_rows")
+        query_rows = load_rows(query, "query_rows")
         val_word_pool = load_words(vals_words, "val_word_pool")
-        load_scales(nc.sync, val_scale_pool, vals_scales)
+        load_scales(val_scale_pool, vals_scales)
         dquery_rows = load_rows(dquery, "dquery_rows")
         gout_rows = load_rows(gout, "gout_rows")
-        reserve_col = column("reserve_col")
+        reserve_col = columns("reserve_col")
         nc.sync.dma_start(out=reserve_col[:], in_=reserve)
-        base_rows = sb.tile([P, T], F32, name="base_rows", align_bytes=64)
+        base_rows = sb.tile([P, TOKENS], F32, name="base_rows", align_bytes=64)
         nc.sync.dma_start(out=base_rows[:], in_=base)
 
-        key_words = gather(key_word_pool, U16, "key_words")
-        key_scales = gather(key_scale_pool, U8, "key_scales")
-        query_mx = quantize(weave(query_rows, "query"), "query")
-        pquery_mx = quantize(weave(pquery_rows, "pquery"), "pquery")
+        key_words = gather(key_word_pool, U16, "key_words", "key_words")
+        key_scales = gather(key_scale_pool, U8, "key_scales", "key_scales")
         pages_bf = sb.tile([P, PAGES, PACK], BF16, name="pages_bf", align_bytes=64)
         for t in range(PACK):
             nc.vector.tensor_copy(pages_bf[:, :, t], pgsum_rows[:, t, :].indirect(page_list[:]))
-
+        pquery_mx = quantize(weave(pquery_rows, "pquery"), "pquery")
         page_codes, page_scales = quantize(pages_bf, "pages")
-        a = product(query_mx, key_words[:].bitcast(FP4X4), key_scales, "a")
         h0 = product(pquery_mx, page_codes[:].bitcast(FP8X4), page_scales, "h0")
+        a = product(quantize(weave(query_rows, "query"), "query"), key_words[:].bitcast(FP4X4), key_scales, "a")
+        val_words = gather(val_word_pool, U16, "val_words", "query_bf")
 
-        val_words = gather(val_word_pool, U16, "val_words")
-        val_scales = gather(val_scale_pool, U8, "val_scales")
-
-        exp_a = wide("exp_a")
-        nc.scalar.activation(exp_a[:], a[:], ACT.Exp)
-        dquery_bf = weave(dquery_rows, "dquery")
-        gout_bf = weave(gout_rows, "gout")
-        h_abs = column("h_abs", PAGES)
-        h_neg = column("h_neg", PAGES)
-        h_tanh = column("h_tanh", PAGES)
-        h_exp = sb.tile([P, PAGES], F32, name="h_exp", tag="gout_rows", align_bytes=64)
+        h_abs = columns("h_abs", PAGES)
+        h_neg = columns("h_neg", PAGES)
+        h_tanh = columns("h_tanh", PAGES)
+        h_exp = columns("h_exp", PAGES)
         nc.scalar.activation(h_abs[:], h0[:], ACT.Abs)
         nc.scalar.activation(h_neg[:], h0[:], ACT.Relu, scale=-1.0)
         nc.scalar.activation(h_tanh[:], h_abs[:], ACT.Tanh, scale=0.5)
         nc.scalar.activation(h_exp[:], h_neg[:], ACT.Exp, scale=-1.0)
-        reserve_scaled = column("reserve_scaled")
-        nc.scalar.activation(reserve_scaled[:], reserve_col[:], ACT.Copy, scale=2.0 / GAIN)
-
-        ta = product(quantize(dquery_bf, "dquery"), key_words[:].bitcast(FP4X4), key_scales, "ta")
-        c0 = product(quantize(gout_bf, "gout"), val_words[:].bitcast(FP4X4), val_scales, "c0")
-
-        gate2 = column("gate2", PAGES)
+        gate2 = columns("gate2", PAGES)
         nc.vector.scalar_tensor_tensor(gate2[:], h_tanh[:], 1.0, h_exp[:], ALU.add, ALU.mult)
-        p2 = wide("p2")
-        p2_sum = column("p2_sum")
+
+        val_scales = gather(val_scale_pool, U8, "val_scales", "val_scales")
+        ta = product(quantize(weave(dquery_rows, "dquery"), "dquery"), key_words[:].bitcast(FP4X4), key_scales, "ta")
+        c0 = product(quantize(weave(gout_rows, "gout"), "gout"), val_words[:].bitcast(FP4X4), val_scales, "c0")
+        exp_a = sb.tile([P, SLOTS], F32, name="exp_a", tag="gout_rows", align_bytes=64)
+        nc.scalar.activation(exp_a[:], a[:], ACT.Exp)
+
+        p2 = by_slot("p2")
+        p2_sum = columns("p2_sum")
         nc.vector.scalar_tensor_tensor(
             p2[:].rearrange("p (g j) -> p g j", j=PAGE_SLOTS), exp_a[:].rearrange("p (g j) -> p g j", j=PAGE_SLOTS), 1.0,
             gate2[:].unsqueeze(2).to_broadcast([P, PAGES, PAGE_SLOTS]), ALU.mult, ALU.mult, accum_out=p2_sum[:])
-
-        z_scaled = column("z_scaled")
-        nc.scalar.activation(z_scaled[:], p2_sum[:], ACT.Identity, scale=1.0 / GAIN, bias=reserve_scaled[:])
-        tp = wide("tp")
-        nc.vector.scalar_tensor_tensor(tp[:], ta[:], 1.0 / GAIN, p2[:], ALU.mult, ALU.mult, accum_out=tz_pair[:, 0:1])
-        row = column("row", 3)
-        s, mu, neg_rz = row[:, 0:1], row[:, 1:2], row[:, 2:3]
-        nc.vector.reciprocal(s, z_scaled[:])
-        nc.scalar.activation(row[:, 1:3], tz_pair[:], ACT.Copy, scale=s)
-        pc = wide("pc")
-        nu = column("nu")
-        nc.vector.scalar_tensor_tensor(pc[:], c0[:], s, p2[:], ALU.mult, ALU.mult, accum_out=nu[:])
-        by_nu = column("by_nu", 2)
-        nc.scalar.activation(by_nu[:], row[:, 0:2], ACT.Copy, scale=nu[:])
-        tp_nu = wide("tp_nu")
-        nc.scalar.activation(tp_nu[:], tp[:], ACT.Copy, scale=by_nu[:, 0:1])
-        cross = wide("cross")
-        cross_sum = column("cross_sum")
-        nc.vector.scalar_tensor_tensor(cross[:], ta[:], mu, pc[:], ALU.subtract, ALU.mult, accum_out=cross_sum[:])
-        kappa = column("kappa")
-        nc.vector.tensor_scalar(kappa[:], cross_sum[:], by_nu[:, 1:2], neg_rz, ALU.subtract, ALU.mult)
-        rest = wide("rest")
-        nc.vector.scalar_tensor_tensor(rest[:], p2[:], kappa[:], tp_nu[:], ALU.mult, ALU.subtract)
+        z2 = columns("z2")
+        nc.scalar.activation(z2[:], reserve_col[:], ACT.Identity, scale=2.0, bias=p2_sum[:])
+        tp2 = by_slot("tp2")
+        nc.vector.scalar_tensor_tensor(tp2[:], ta[:], 1.0, p2[:], ALU.mult, ALU.mult, accum_out=tz_row[:, 0:1])
+        over_z2 = columns("over_z2", 4)
+        inv_z2, mu, neg_inv_z2, row_gain = over_z2[:, 0:1], over_z2[:, 1:2], over_z2[:, 2:3], over_z2[:, 3:4]
+        nc.vector.reciprocal(inv_z2, z2[:])
+        nc.scalar.activation(over_z2[:, 1:4], tz_row[:], ACT.Copy, scale=inv_z2)
+        cp2 = by_slot("cp2")
+        cp2_sum = columns("cp2_sum")
+        nc.vector.scalar_tensor_tensor(cp2[:], c0[:], 1.0, p2[:], ALU.mult, ALU.mult, accum_out=cp2_sum[:])
+        times_cp2_sum = columns("times_cp2_sum", 2)
+        nu, mu_cp2_sum = times_cp2_sum[:, 0:1], times_cp2_sum[:, 1:2]
+        nc.scalar.activation(times_cp2_sum[:], over_z2[:, 0:2], ACT.Copy, scale=cp2_sum[:])
+        nu_tp2 = by_slot("nu_tp2")
+        nc.scalar.activation(nu_tp2[:], tp2[:], ACT.Copy, scale=nu)
+        cross = by_slot("cross")
+        cross_sum = columns("cross_sum")
+        nc.vector.scalar_tensor_tensor(cross[:], ta[:], mu, cp2[:], ALU.subtract, ALU.mult, accum_out=cross_sum[:])
+        kappa = columns("kappa")
+        nc.vector.tensor_scalar(kappa[:], cross_sum[:], mu_cp2_sum, neg_inv_z2, ALU.subtract, ALU.mult)
+        rest = by_slot("rest")
+        nc.vector.scalar_tensor_tensor(rest[:], p2[:], kappa[:], nu_tp2[:], ALU.mult, ALU.subtract)
         nc.vector.tensor_tensor(scattered[:].indirect(slot_list[:]), cross[:], rest[:], ALU.add)
 
         start = 0
         for n, width in enumerate(STORE_WIDTHS):
             cols = slice(start, start + width)
             result = sb.tile([P, width], F32, name="result%d" % n, align_bytes=64)
-            nc.vector.tensor_tensor(result[:], base_rows[:, cols], scattered[:, cols], ALU.add)
+            nc.vector.scalar_tensor_tensor(result[:], scattered[:, cols], row_gain, base_rows[:, cols], ALU.mult, ALU.add)
             nc.sync.dma_start(out=out[:, cols], in_=result[:])
             start = start + width

@@ -57,13 +57,13 @@ def tile_attend_hvpagetablegate_s_kernel(tc, query, pquery, keys_words, keys_sca
             nc.sync.dma_start(out=tile[:], in_=rows.rearrange("(p t) c -> p t c", t=PACK))
             return tile
 
-        def gather(window, dtype, name, tag):
-            tile = sb.tile([P, SLOTS], dtype, name=name, tag=tag, align_bytes=64)
+        def gather(window, dtype, name):
+            tile = sb.tile([P, SLOTS], dtype, name=name, align_bytes=64)
             nc.vector.tensor_copy(tile[:], window[:].indirect(slot_list[:]))
             return tile
 
         def weave(planes, name):
-            woven = sb.tile([P, planes.shape[2], PACK], BF16, name=name + "_bf", tag=name + "_bf", align_bytes=64)
+            woven = sb.tile([P, planes.shape[2], PACK], BF16, name=name + "_bf", align_bytes=64)
             nc.scalar.copy(out=woven[:].rearrange("p (c i) t -> p c t i", i=RUN),
                            in_=planes[:].rearrange("p t (c i) -> p c t i", i=RUN))
             return woven
@@ -91,11 +91,11 @@ def tile_attend_hvpagetablegate_s_kernel(tc, query, pquery, keys_words, keys_sca
 
         key_scale_pool = zeroed_scales("key_scale_pool")
         val_scale_pool = zeroed_scales("val_scale_pool")
+        tz_row = columns("tz_row", 3)
+        nc.vector.memset(tz_row[:, 2:3], GAIN)
+        nc.scalar.activation(tz_row[:, 1:2], tz_row[:, 2:3], ACT.Copy, scale=-1.0 / GAIN)
         scattered = sb.tile([P, TOKENS], F32, name="scattered", align_bytes=64)
         nc.vector.memset(scattered[:], 0.0)
-        tz_row = columns("tz_row", 3)
-        nc.vector.memset(tz_row[:, 1:2], -1.0)
-        nc.vector.memset(tz_row[:, 2:3], GAIN)
 
         slot_list = sb.tile([P, SLOTS // LIST_ROWS], U16, name="slot_list")
         nc.sync.dma_start(slot_list[:], offs)
@@ -115,8 +115,8 @@ def tile_attend_hvpagetablegate_s_kernel(tc, query, pquery, keys_words, keys_sca
         base_rows = sb.tile([P, TOKENS], F32, name="base_rows", align_bytes=64)
         nc.sync.dma_start(out=base_rows[:], in_=base)
 
-        key_words = gather(key_word_pool, U16, "key_words", "key_words")
-        key_scales = gather(key_scale_pool, U8, "key_scales", "key_scales")
+        key_words = gather(key_word_pool, U16, "key_words")
+        key_scales = gather(key_scale_pool, U8, "key_scales")
         pages_bf = sb.tile([P, PAGES, PACK], BF16, name="pages_bf", align_bytes=64)
         for t in range(PACK):
             nc.vector.tensor_copy(pages_bf[:, :, t], pgsum_rows[:, t, :].indirect(page_list[:]))
@@ -124,7 +124,7 @@ def tile_attend_hvpagetablegate_s_kernel(tc, query, pquery, keys_words, keys_sca
         page_codes, page_scales = quantize(pages_bf, "pages")
         h0 = product(pquery_mx, page_codes[:].bitcast(FP8X4), page_scales, "h0")
         a = product(quantize(weave(query_rows, "query"), "query"), key_words[:].bitcast(FP4X4), key_scales, "a")
-        val_words = gather(val_word_pool, U16, "val_words", "query_bf")
+        val_words = gather(val_word_pool, U16, "val_words")
 
         h_abs = columns("h_abs", PAGES)
         h_neg = columns("h_neg", PAGES)
@@ -137,7 +137,7 @@ def tile_attend_hvpagetablegate_s_kernel(tc, query, pquery, keys_words, keys_sca
         gate2 = columns("gate2", PAGES)
         nc.vector.scalar_tensor_tensor(gate2[:], h_tanh[:], 1.0, h_exp[:], ALU.add, ALU.mult)
 
-        val_scales = gather(val_scale_pool, U8, "val_scales", "val_scales")
+        val_scales = gather(val_scale_pool, U8, "val_scales")
         ta = product(quantize(weave(dquery_rows, "dquery"), "dquery"), key_words[:].bitcast(FP4X4), key_scales, "ta")
         c0 = product(quantize(weave(gout_rows, "gout"), "gout"), val_words[:].bitcast(FP4X4), val_scales, "c0")
         exp_a = sb.tile([P, SLOTS], F32, name="exp_a", tag="gout_rows", align_bytes=64)

from contextlib import ExitStack

import concourse.mybir as mybir

F32 = mybir.dt.float32
BF16 = mybir.dt.bfloat16
I32 = mybir.dt.int32
U32 = mybir.dt.uint32
U16 = mybir.dt.uint16
U8 = mybir.dt.uint8
FP8X4 = mybir.dt.float8_e4m3fn_x4
FP4X4 = mybir.dt.float4_e2m1fn_x4
ACT = mybir.ActivationFunctionType
ALU = mybir.AluOpType

P = 128
PACK = 4
K = P * PACK
BLOCKS = K // 32
QUADRANT = 32
LIST_ROWS = 16
RUN = 4
TOKENS = 2048
SLOTS = 512
PAGES = 64
PAGE_SLOTS = SLOTS // PAGES
GAIN = 512.0
STORE_WIDTHS = (256, 512, 512, 512, 256)

FLOPS = 2 * K * P * (3 * SLOTS + PAGES)


def tile_attend_hvpagetablegate_s_kernel(tc, query, pquery, keys_words, keys_scales, pgsum, reserve, gout,
                                          vals_words, vals_scales, dquery, base, offs2, offs, out):
    nc = tc.nc
    with ExitStack() as ctx:
        sb = ctx.enter_context(tc.tile_pool(name="sb", bufs=1))
        ps = ctx.enter_context(tc.psum_pool(name="ps", bufs=1))

        def load_words(words, name):
            tile = sb.tile([P, TOKENS], U16, name=name, align_bytes=64)
            nc.sync.dma_start(out=tile[:].bitcast(I32), in_=words[0].bitcast(I32))
            return tile

        def zeroed_scales(name):
            tile = sb.tile([P, TOKENS], U8, name=name, tag=name, align_bytes=64)
            nc.gpsimd.memset(tile[:].bitcast(I32), 0)
            return tile

        def load_scales(tile, scales):
            for r in range(PACK):
                nc.sync.dma_start(out=tile[:].bitcast(I32)[r:P:QUADRANT, :],
                                  in_=scales[0].bitcast(I32)[r:BLOCKS:PACK, :])

        def load_rows(rows, name):
            tile = sb.tile([P, PACK, rows.shape[1]], F32, name=name, tag=name, align_bytes=64)
            nc.sync.dma_start(out=tile[:], in_=rows.rearrange("(p t) c -> p t c", t=PACK))
            return tile

        def gather(window, dtype, name):
            tile = sb.tile([P, SLOTS], dtype, name=name, align_bytes=64)
            nc.vector.tensor_copy(tile[:], window[:].indirect(slot_list[:]))
            return tile

        def weave(planes, name):
            woven = sb.tile([P, planes.shape[2], PACK], BF16, name=name + "_bf", align_bytes=64)
            nc.scalar.copy(out=woven[:].rearrange("p (c i) t -> p c t i", i=RUN),
                           in_=planes[:].rearrange("p t (c i) -> p c t i", i=RUN))
            return woven

        def quantize(woven, name):
            width = woven.shape[1]
            codes = sb.tile([P, width], U32, name=name + "_codes", align_bytes=64)
            scales = sb.tile([P, width], U8, name=name + "_scales", align_bytes=64)
            nc.vector.quantize_mx(out=codes[:].bitcast(FP8X4), scales=scales[:],
                                  in_=woven[:].rearrange("p c t -> p (c t)"))
            return codes, scales

        def product(stationary, moving, moving_scales, name):
            codes, scales = stationary
            acc = ps.tile([P, moving_scales.shape[1]], F32, name=name)
            nc.tensor.matmul_mx(out=acc[:], lhsT=codes[:].bitcast(FP8X4), lhsT_scale=scales[:],
                                rhs=moving, rhs_scale=moving_scales[:], start=True, stop=True)
            return acc

        def by_slot(name):
            return sb.tile([P, SLOTS], F32, name=name, align_bytes=64)

        def columns(name, n=1):
            return sb.tile([P, n], F32, name=name)

        key_scale_pool = zeroed_scales("key_scale_pool")
        val_scale_pool = zeroed_scales("val_scale_pool")
        tz_row = columns("tz_row", 3)
        nc.vector.memset(tz_row[:, 2:3], GAIN)
        nc.scalar.activation(tz_row[:, 1:2], tz_row[:, 2:3], ACT.Copy, scale=-1.0 / GAIN)
        scattered = sb.tile([P, TOKENS], F32, name="scattered", align_bytes=64)
        nc.vector.memset(scattered[:], 0.0)

        slot_list = sb.tile([P, SLOTS // LIST_ROWS], U16, name="slot_list")
        nc.sync.dma_start(slot_list[:], offs)
        key_word_pool = load_words(keys_words, "key_word_pool")
        load_scales(key_scale_pool, keys_scales)
        pgsum_rows = load_rows(pgsum, "pgsum_rows")
        page_list = sb.tile([P, PAGES // LIST_ROWS], U16, name="page_list")
        nc.sync.dma_start(page_list[:], offs2)
        pquery_rows = load_rows(pquery, "pquery_rows")
        query_rows = load_rows(query, "query_rows")
        val_word_pool = load_words(vals_words, "val_word_pool")
        load_scales(val_scale_pool, vals_scales)
        dquery_rows = load_rows(dquery, "dquery_rows")
        gout_rows = load_rows(gout, "gout_rows")
        reserve_col = columns("reserve_col")
        nc.sync.dma_start(out=reserve_col[:], in_=reserve)
        base_rows = sb.tile([P, TOKENS], F32, name="base_rows", align_bytes=64)
        nc.sync.dma_start(out=base_rows[:], in_=base)

        key_words = gather(key_word_pool, U16, "key_words")
        key_scales = gather(key_scale_pool, U8, "key_scales")
        pages_bf = sb.tile([P, PAGES, PACK], BF16, name="pages_bf", align_bytes=64)
        for t in range(PACK):
            nc.vector.tensor_copy(pages_bf[:, :, t], pgsum_rows[:, t, :].indirect(page_list[:]))
        pquery_mx = quantize(weave(pquery_rows, "pquery"), "pquery")
        page_codes, page_scales = quantize(pages_bf, "pages")
        h0 = product(pquery_mx, page_codes[:].bitcast(FP8X4), page_scales, "h0")
        a = product(quantize(weave(query_rows, "query"), "query"), key_words[:].bitcast(FP4X4), key_scales, "a")
        val_words = gather(val_word_pool, U16, "val_words")

        h_abs = columns("h_abs", PAGES)
        h_neg = columns("h_neg", PAGES)
        h_tanh = columns("h_tanh", PAGES)
        h_exp = columns("h_exp", PAGES)
        nc.scalar.activation(h_abs[:], h0[:], ACT.Abs)
        nc.scalar.activation(h_neg[:], h0[:], ACT.Relu, scale=-1.0)
        nc.scalar.activation(h_tanh[:], h_abs[:], ACT.Tanh, scale=0.5)
        nc.scalar.activation(h_exp[:], h_neg[:], ACT.Exp, scale=-1.0)
        gate2 = columns("gate2", PAGES)
        nc.vector.scalar_tensor_tensor(gate2[:], h_tanh[:], 1.0, h_exp[:], ALU.add, ALU.mult)

        val_scales = gather(val_scale_pool, U8, "val_scales")
        ta = product(quantize(weave(dquery_rows, "dquery"), "dquery"), key_words[:].bitcast(FP4X4), key_scales, "ta")
        c0 = product(quantize(weave(gout_rows, "gout"), "gout"), val_words[:].bitcast(FP4X4), val_scales, "c0")
        exp_a = sb.tile([P, SLOTS], F32, name="exp_a", tag="gout_rows", align_bytes=64)
        nc.scalar.activation(exp_a[:], a[:], ACT.Exp)

        p2 = by_slot("p2")
        p2_sum = columns("p2_sum")
        nc.vector.scalar_tensor_tensor(
            p2[:].rearrange("p (g j) -> p g j", j=PAGE_SLOTS), exp_a[:].rearrange("p (g j) -> p g j", j=PAGE_SLOTS), 1.0,
            gate2[:].unsqueeze(2).to_broadcast([P, PAGES, PAGE_SLOTS]), ALU.mult, ALU.mult, accum_out=p2_sum[:])
        z2 = columns("z2")
        nc.scalar.activation(z2[:], reserve_col[:], ACT.Identity, scale=2.0, bias=p2_sum[:])
        tp2 = by_slot("tp2")
        nc.vector.scalar_tensor_tensor(tp2[:], ta[:], 1.0, p2[:], ALU.mult, ALU.mult, accum_out=tz_row[:, 0:1])
        over_z2 = columns("over_z2", 4)
        inv_z2, mu, neg_inv_z2, row_gain = over_z2[:, 0:1], over_z2[:, 1:2], over_z2[:, 2:3], over_z2[:, 3:4]
        nc.vector.reciprocal(inv_z2, z2[:])
        nc.scalar.activation(over_z2[:, 1:4], tz_row[:], ACT.Copy, scale=inv_z2)
        cp2 = by_slot("cp2")
        cp2_sum = columns("cp2_sum")
        nc.vector.scalar_tensor_tensor(cp2[:], c0[:], 1.0, p2[:], ALU.mult, ALU.mult, accum_out=cp2_sum[:])
        times_cp2_sum = columns("times_cp2_sum", 2)
        nu, mu_cp2_sum = times_cp2_sum[:, 0:1], times_cp2_sum[:, 1:2]
        nc.scalar.activation(times_cp2_sum[:], over_z2[:, 0:2], ACT.Copy, scale=cp2_sum[:])
        nu_tp2 = by_slot("nu_tp2")
        nc.scalar.activation(nu_tp2[:], tp2[:], ACT.Copy, scale=nu)
        cross = by_slot("cross")
        cross_sum = columns("cross_sum")
        nc.vector.scalar_tensor_tensor(cross[:], ta[:], mu, cp2[:], ALU.subtract, ALU.mult, accum_out=cross_sum[:])
        kappa = columns("kappa")
        nc.vector.tensor_scalar(kappa[:], cross_sum[:], mu_cp2_sum, neg_inv_z2, ALU.subtract, ALU.mult)
        rest = by_slot("rest")
        nc.vector.scalar_tensor_tensor(rest[:], p2[:], kappa[:], nu_tp2[:], ALU.mult, ALU.subtract)
        nc.vector.tensor_tensor(scattered[:].indirect(slot_list[:]), cross[:], rest[:], ALU.add)

        start = 0
        for n, width in enumerate(STORE_WIDTHS):
            cols = slice(start, start + width)
            result = sb.tile([P, width], F32, name="result%d" % n, align_bytes=64)
            nc.vector.scalar_tensor_tensor(result[:], scattered[:, cols], row_gain, base_rows[:, cols], ALU.mult, ALU.add)
            nc.sync.dma_start(out=out[:, cols], in_=result[:])
            start = start + width
